import numpy as np
import ml_dtypes


def mxq(x, axis, fmt="e4m3"):
    dtype, down = {"e4m3": (ml_dtypes.float8_e4m3fn, 7), "e5m2": (ml_dtypes.float8_e5m2, 14)}[fmt]
    v = np.moveaxis(np.asarray(x, np.float32).astype(ml_dtypes.bfloat16).astype(np.float64), axis, -1)
    blocks = v.reshape(v.shape[:-1] + (-1, 32))
    amax = np.abs(blocks).max(-1, keepdims=True)
    byte = np.maximum(np.where(amax > 0, np.frexp(amax)[1] - 1 + 127, 0) - down, 1)
    scale = np.exp2(byte - 127.0)
    codes = (blocks / scale).astype(np.float32).astype(dtype).astype(np.float64)
    return np.moveaxis((codes * scale).reshape(v.shape), -1, axis)


WIDE = False


def mx_kscale(k):
    if not WIDE:
        return np.ones(k)
    levels = np.array([10, -10, 5, -5, 0])
    if k % 512:
        return np.exp2(np.random.permutation(np.resize(levels, k // 32))).repeat(32)
    a = np.empty((k // 512, 16))
    for p in range(k // 512):
        a[p, :8] = np.random.permutation(np.resize(levels, 8))
        for g in range(8):
            far = levels[np.abs(levels - a[p, g]) >= 10]
            a[p, g + 8] = far[np.random.randint(len(far))]
    return np.exp2(a.ravel()).repeat(32)


def f64(x):
    return np.asarray(x).astype(np.float64)


def striped(idx):
    return np.tile(np.asarray(idx).reshape(-1, 16).T, (8, 1)).astype(np.uint16)


def unstriped(offs):
    return offs[:16].T.reshape(-1).astype(np.int64)


E2M1 = np.array([0.0, 0.5, 1.0, 1.5, 2.0, 3.0, 4.0, 6.0, -0.0, -0.5, -1.0, -1.5, -2.0, -3.0, -4.0, -6.0])


def pack_weight(w, fmt):
    k, n = w.shape
    w = f64(np.asarray(w, np.float32).astype(ml_dtypes.bfloat16)).reshape(k // 32, 32, n)
    amax = np.abs(w).max(1)
    if fmt == "e4m3":
        byte = np.frexp(amax)[1] - 1 + 127 - 7
    else:
        mant, ex = np.frexp(amax / 6.0)
        byte = np.where(mant > 0.5, ex, ex - 1) + 127
    byte = np.clip(np.where(amax > 0, byte, 1), 1, 254)
    scaled = (w * np.exp2(127.0 - byte)[:, None, :]).reshape(k, n).astype(np.float32)
    by_word = np.ascontiguousarray(scaled.reshape(k // 512, 128, 4, n).transpose(0, 1, 3, 2))
    if fmt == "e4m3":
        words = by_word.astype(ml_dtypes.float8_e4m3fn).view(np.uint8)
    else:
        c = by_word.astype(ml_dtypes.float4_e2m1fn).view(np.uint8) & 0xF
        words = (c[..., 0::2] | (c[..., 1::2] << 4)).reshape(k // 512, 128, 2 * n)
    return np.ascontiguousarray(words), np.ascontiguousarray(byte.astype(np.uint8).reshape(k // 512, 16, n))


def unpack_weight(words, scales, fmt):
    g, _, n = scales.shape
    words = np.ascontiguousarray(words).reshape(g, 128, n, -1)
    if fmt == "e4m3":
        vals = words.view(ml_dtypes.float8_e4m3fn).astype(np.float64)
    else:
        nib = np.empty((g, 128, n, 4), np.uint8)
        nib[..., 0::2] = words & 0xF
        nib[..., 1::2] = words >> 4
        vals = E2M1[nib]
    vals = vals * np.repeat(np.exp2(scales.astype(np.float64) - 127.0), 8, axis=1)[..., None]
    return vals.transpose(0, 1, 3, 2).reshape(g * 512, n)


def sigmoid(v):
    return 1.0 / (1.0 + np.exp(-v))


def sgn(shape):
    return np.random.uniform(0.5, 2.0, shape) * np.where(np.random.standard_normal(shape) < 0, -1.0, 1.0)


K, T, J, R, F, Z, C, O, U = 512, 1024, 256, 512, 512, 1024, 512, 128, 128


def setup_inputs():
    n = np.random.standard_normal
    idx = np.random.permutation(T)[:J]
    idx2 = np.random.permutation(Z)[:J]
    idx3 = np.random.permutation(J)[:O]
    idx4 = np.random.permutation(C)[:J]
    idx5 = np.random.permutation(C)[:U]
    fk = mx_kscale(K)
    ff = mx_kscale(F)
    fr = mx_kscale(R)
    fr = fr / fr.max()
    xtp = pack_weight(n((K, T)) / fk[:, None], "e4m3")
    xop = pack_weight(n((F, Z)) / ff[:, None], "e4m3")
    wp = pack_weight(n((K, R)) * 1 / np.sqrt(K) * fk[:, None], "e2m1")
    w2p = pack_weight(n((F, R)) * 1 / np.sqrt(F) * ff[:, None], "e2m1")
    return {
        "xt_words": xtp[0],
        "xt_scales": xtp[1],
        "xo_words": xop[0],
        "xo_scales": xop[1],
        "w_words": wp[0],
        "w_scales": wp[1],
        "w2_words": w2p[0],
        "w2_scales": w2p[1],
        "sg": (0.3 * sgn((R, 1))).astype(np.float32),
        "lo": (np.random.uniform(-1.0, 0.6, (R, 1)) + np.log(fr)[:, None]).astype(np.float32),
        "sb": (sgn((R, 1)) / fr[:, None] / np.sqrt(R)).astype(np.float32),
        "offs": striped(idx),
        "offs2": striped(idx2),
        "offs3": striped(idx3),
        "offs4": striped(idx4),
        "offs5": striped(idx5),
    }


def reference(xt_words, xt_scales, xo_words, xo_scales, w_words, w_scales, w2_words, w2_scales, sg, lo, sb, offs, offs2, offs3, offs4, offs5):
    idx = unstriped(offs)
    idx2 = unstriped(offs2)
    idx3 = unstriped(offs3)
    idx4 = unstriped(offs4)
    idx5 = unstriped(offs5)
    xtu = unpack_weight(xt_words, xt_scales, "e4m3")
    xou = unpack_weight(xo_words, xo_scales, "e4m3")
    wu = unpack_weight(w_words, w_scales, "e2m1")
    w2u = unpack_weight(w2_words, w2_scales, "e2m1")
    xtidxg = xtu[:, idx]
    a = wu.T @ xtidxg
    xoidx2g = xou[:, idx2]
    b = w2u.T @ xoidx2g
    z1 = sigmoid(a[:, idx3] * f64(sg) + f64(lo))
    pw = np.zeros((R, C))
    pw[:, idx4] = b * f64(sb)
    z2 = pw[:, idx5]
    z1q = mxq(z1, 0, "e4m3")
    z2q = mxq(z2, 0, "e4m3")
    y = z1q.T @ z2q
    return y

@@ -1,0 +1,174 @@
+from contextlib import ExitStack
+
+import concourse.mybir as mybir
+
+K, T, J, R, C, O, U = 512, 1024, 256, 512, 512, 128, 128
+FLOPS = 2 * (2 * K * R * J + R * O * U)
+
+F32 = mybir.dt.float32
+BF16 = mybir.dt.bfloat16
+I32 = mybir.dt.int32
+U32 = mybir.dt.uint32
+U16 = mybir.dt.uint16
+U8 = mybir.dt.uint8
+FP8X4 = mybir.dt.float8_e4m3fn_x4
+FP4X4 = mybir.dt.float4_e2m1fn_x4
+ACT = mybir.ActivationFunctionType
+
+P = 128
+PACK = 4
+QUADS = 4
+HALF = J // 2
+
+
+def tile_list_softpairs_kernel(tc, xt_words, xt_scales, xo_words, xo_scales, w_words, w_scales, w2_words, w2_scales,
+                                   sg, lo, sb, offs, offs2, offs3, offs4, offs5, out):
+    nc = tc.nc
+    with ExitStack() as ctx:
+        pool = ctx.enter_context(tc.tile_pool(name="sbuf", bufs=1))
+        psum = ctx.enter_context(tc.psum_pool(name="psum", bufs=1))
+
+        def sbuf(name, cols, dtype, rows=P):
+            return pool.tile([rows, cols], dtype, name=name, align_bytes=64)
+
+        def load_list(name, src):
+            tile = pool.tile([P, src.shape[1]], U16, name=name)
+            nc.sync.dma_start(tile[:], src)
+            return tile
+
+        def load_words(name, queue, src, cols, dtype):
+            tile = sbuf(name, cols, dtype)
+            queue.dma_start(tile[:].bitcast(I32), src.bitcast(I32))
+            return tile
+
+        def load_scale_rows(name, queue, src):
+            words = src.shape[2] // 4
+            tile = sbuf(name, QUADS * words, I32, rows=4)
+            queue.dma_start(tile[:].rearrange("r (q n) -> r q n", q=QUADS),
+                            src[0].bitcast(I32).rearrange("(q r) n -> r q n", q=QUADS))
+            return tile
+
+        def load_columns(name, queue, src):
+            tile = sbuf(name, PACK, F32)
+            queue.dma_start(tile[:], src.rearrange("(p t) o -> p (t o)", t=PACK))
+            return tile
+
+        def zeroed_plane(name, cols):
+            plane = sbuf(name, cols, U8)
+            nc.vector.memset(plane[:].bitcast(I32), 0)
+            return plane
+
+        def spread(plane, rows):
+            words = plane.shape[1] // 4
+            for q in range(QUADS):
+                nc.vector.tensor_copy(plane[32 * q:32 * q + 4, :].bitcast(I32), rows[:, q * words:(q + 1) * words])
+
+        def dealt(tile):
+            return tile[:].rearrange("p (t m) -> p t m", t=PACK)
+
+        def undealt(tile):
+            return tile[:].rearrange("p (m t) -> p t m", t=PACK)
+
+        def load_plane(plane, src):
+            for q in range(QUADS):
+                nc.sync.dma_start(plane[32 * q:32 * q + 4, :].bitcast(I32), src[0, 4 * q:4 * q + 4, :].bitcast(I32))
+
+        xo_plane = zeroed_plane("xo_plane", T)
+        w2_plane = zeroed_plane("w2_plane", R)
+        boards = [sbuf("board%d" % t, C, F32) for t in range(PACK)]
+        for t in range(PACK):
+            nc.vector.memset(boards[t][:], 0.0)
+        xt_plane = zeroed_plane("xt_plane", T)
+        w_plane = zeroed_plane("w_plane", R)
+
+        xo_w = load_words("xo_w", nc.scalar, xo_words[0].rearrange("p n t -> p (n t)"), T, U32)
+        w2_rows = load_scale_rows("w2_rows", nc.sync, w2_scales)
+        l2 = load_list("l2", offs2)
+        w2_raw = load_words("w2_raw", nc.sync, w2_words[0], R, U16)
+        load_plane(xo_plane, xo_scales)
+        l4 = load_list("l4", offs4)
+        sb_t = load_columns("sb_t", nc.sync, sb)
+        xt_w = load_words("xt_w", nc.sync, xt_words[0].rearrange("p n t -> p (n t)"), T, U32)
+        w_raw = load_words("w_raw", nc.sync, w_words[0], R, U16)
+        l1 = load_list("l1", offs)
+        load_plane(xt_plane, xt_scales)
+        w_rows = load_scale_rows("w_rows", nc.sync, w_scales)
+        sg_t = load_columns("sg_t", nc.sync, sg)
+        lo_t = load_columns("lo_t", nc.sync, lo)
+        l3 = load_list("l3", offs3)
+        l5 = load_list("l5", offs5)
+
+        w2_d = sbuf("w2_d", R, U16)
+        nc.scalar.copy(dealt(w2_d), undealt(w2_raw))
+        w2_s = sbuf("w2_s", R, U8)
+        xo_gw = sbuf("xo_gw", J, U32)
+        xo_gs = sbuf("xo_gs", J, U8)
+
+        def gather_half(dst, window, lst, h):
+            nc.vector.tensor_copy(dst[:, h * HALF:(h + 1) * HALF],
+                                  window[:].indirect(lst[:, h * HALF // 16:(h + 1) * HALF // 16]))
+
+        def put(name, t, c0, c1):
+            acc = psum.tile([P, c1 - c0], F32, name="acc_" + name)
+            nc.tensor.matmul_mx(out=acc[:], lhsT=w2_d[:, t * P:(t + 1) * P].bitcast(FP4X4), lhsT_scale=w2_s[:, t * P:(t + 1) * P],
+                                rhs=xo_gw[:, c0:c1].bitcast(FP8X4), rhs_scale=xo_gs[:, c0:c1], start=True, stop=True)
+            b = sbuf("b_" + name, c1 - c0, F32)
+            nc.vector.tensor_copy(b[:], acc[:])
+            nc.scalar.activation(out=boards[t][:].indirect(l4[:, c0 // 16:c1 // 16]), in_=b[:], func=ACT.Copy,
+                                 scale=sb_t[:, t:t + 1])
+
+        def deal_scales(t):
+            nc.vector.tensor_copy(w2_s[:, t * P:(t + 1) * P], w2_plane[:, t::PACK])
+
+        spread(w2_plane, w2_rows)
+        gather_half(xo_gs, xo_plane, l2, 0)
+        deal_scales(0)
+        gather_half(xo_gw, xo_w, l2, 0)
+        deal_scales(1)
+        put("0a", 0, 0, HALF)
+        put("1a", 1, 0, HALF)
+        gather_half(xo_gs, xo_plane, l2, 1)
+        gather_half(xo_gw, xo_w, l2, 1)
+        put("0b", 0, HALF, J)
+        put("1b", 1, HALF, J)
+        for t in (2, 3):
+            deal_scales(t)
+            put(str(t), t, 0, J)
+
+        spread(w_plane, w_rows)
+        w_d = sbuf("w_d", R, U16)
+        w_s = sbuf("w_s", R, U8)
+        xt_gw = sbuf("xt_gw", J, U32)
+        xt_gs = sbuf("xt_gs", J, U8)
+        nc.vector.tensor_copy(xt_gs[:], xt_plane[:].indirect(l1[:]))
+        nc.vector.tensor_copy(dealt(w_s), undealt(w_plane))
+        nc.vector.tensor_copy(dealt(w_d), undealt(w_raw))
+        nc.vector.tensor_copy(xt_gw[:], xt_w[:].indirect(l1[:]))
+
+        z1 = sbuf("z1", PACK * O, BF16)
+        z2 = sbuf("z2", PACK * U, BF16)
+        acc_a = [psum.tile([P, 2 * J], F32, name="acc_a%d" % i) for i in range(2)]
+        for t in range(PACK):
+            acc = acc_a[t // 2][:, (t % 2) * J:(t % 2 + 1) * J]
+            nc.tensor.matmul_mx(out=acc, lhsT=w_d[:, t * P:(t + 1) * P].bitcast(FP4X4), lhsT_scale=w_s[:, t * P:(t + 1) * P],
+                                rhs=xt_gw[:].bitcast(FP8X4), rhs_scale=xt_gs[:], start=True, stop=True)
+        for t in range(PACK):
+            a = sbuf("a%d" % t, J, F32)
+            nc.vector.tensor_copy(a[:], acc_a[t // 2][:, (t % 2) * J:(t % 2 + 1) * J])
+            nc.scalar.activation(out=z1[:, t::PACK], in_=a[:].indirect(l3[:]), func=ACT.Sigmoid,
+                                 bias=lo_t[:, t:t + 1], scale=sg_t[:, t:t + 1])
+        for t in range(PACK):
+            nc.scalar.activation(out=z2[:, t::PACK], in_=boards[t][:].indirect(l5[:]), func=ACT.Copy)
+
+        z1_w = sbuf("z1_w", O, U32)
+        z1_s = sbuf("z1_s", O, U8)
+        z2_w = sbuf("z2_w", U, U32)
+        z2_s = sbuf("z2_s", U, U8)
+        nc.vector.quantize_mx(out=z1_w[:].bitcast(FP8X4), scales=z1_s[:], in_=z1[:])
+        nc.vector.quantize_mx(out=z2_w[:].bitcast(FP8X4), scales=z2_s[:], in_=z2[:])
+        acc_y = psum.tile([O, U], F32, name="acc_0a")
+        nc.tensor.matmul_mx(out=acc_y[:], lhsT=z1_w[:].bitcast(FP8X4), lhsT_scale=z1_s[:],
+                            rhs=z2_w[:].bitcast(FP8X4), rhs_scale=z2_s[:], start=True, stop=True)
+        y = sbuf("y", U, F32)
+        nc.vector.tensor_copy(y[:], acc_y[:])
+        nc.sync.dma_start(out, y[:])

@@ -98,6 +98,11 @@ def tile_list_softpairs_kernel(tc, xt_words, xt_scales, xo_words, xo_scales, w_w
         l3 = load_list("l3", offs3)
         l5 = load_list("l5", offs5)
 
+        warm_in = sbuf("warm_in", 1, F32)
+        warm_out = sbuf("warm_out", 1, F32)
+        nc.gpsimd.memset(warm_in[:], 0.0)
+        nc.scalar.activation(out=warm_out[:], in_=warm_in[:], func=ACT.Sigmoid)
+
         w2_d = sbuf("w2_d", R, U16)
         nc.scalar.copy(dealt(w2_d), undealt(w2_raw))
         w2_s = sbuf("w2_s", R, U8)

from contextlib import ExitStack

import concourse.mybir as mybir

K, T, J, R, C, O, U = 512, 1024, 256, 512, 512, 128, 128
FLOPS = 2 * (2 * K * R * J + R * O * U)

F32 = mybir.dt.float32
BF16 = mybir.dt.bfloat16
I32 = mybir.dt.int32
U32 = mybir.dt.uint32
U16 = mybir.dt.uint16
U8 = mybir.dt.uint8
FP8X4 = mybir.dt.float8_e4m3fn_x4
FP4X4 = mybir.dt.float4_e2m1fn_x4
ACT = mybir.ActivationFunctionType

P = 128
PACK = 4
QUADS = 4
HALF = J // 2


def tile_list_softpairs_kernel(tc, xt_words, xt_scales, xo_words, xo_scales, w_words, w_scales, w2_words, w2_scales,
                                   sg, lo, sb, offs, offs2, offs3, offs4, offs5, out):
    nc = tc.nc
    with ExitStack() as ctx:
        pool = ctx.enter_context(tc.tile_pool(name="sbuf", bufs=1))
        psum = ctx.enter_context(tc.psum_pool(name="psum", bufs=1))

        def sbuf(name, cols, dtype, rows=P):
            return pool.tile([rows, cols], dtype, name=name, align_bytes=64)

        def load_list(name, src):
            tile = pool.tile([P, src.shape[1]], U16, name=name)
            nc.sync.dma_start(tile[:], src)
            return tile

        def load_words(name, queue, src, cols, dtype):
            tile = sbuf(name, cols, dtype)
            queue.dma_start(tile[:].bitcast(I32), src.bitcast(I32))
            return tile

        def load_scale_rows(name, queue, src):
            words = src.shape[2] // 4
            tile = sbuf(name, QUADS * words, I32, rows=4)
            queue.dma_start(tile[:].rearrange("r (q n) -> r q n", q=QUADS),
                            src[0].bitcast(I32).rearrange("(q r) n -> r q n", q=QUADS))
            return tile

        def load_columns(name, queue, src):
            tile = sbuf(name, PACK, F32)
            queue.dma_start(tile[:], src.rearrange("(p t) o -> p (t o)", t=PACK))
            return tile

        def zeroed_plane(name, cols):
            plane = sbuf(name, cols, U8)
            nc.vector.memset(plane[:].bitcast(I32), 0)
            return plane

        def spread(plane, rows):
            words = plane.shape[1] // 4
            for q in range(QUADS):
                nc.vector.tensor_copy(plane[32 * q:32 * q + 4, :].bitcast(I32), rows[:, q * words:(q + 1) * words])

        def dealt(tile):
            return tile[:].rearrange("p (t m) -> p t m", t=PACK)

        def undealt(tile):
            return tile[:].rearrange("p (m t) -> p t m", t=PACK)

        def load_plane(plane, src):
            for q in range(QUADS):
                nc.sync.dma_start(plane[32 * q:32 * q + 4, :].bitcast(I32), src[0, 4 * q:4 * q + 4, :].bitcast(I32))

        xo_plane = zeroed_plane("xo_plane", T)
        w2_plane = zeroed_plane("w2_plane", R)
        boards = [sbuf("board%d" % t, C, F32) for t in range(PACK)]
        for t in range(PACK):
            nc.vector.memset(boards[t][:], 0.0)
        xt_plane = zeroed_plane("xt_plane", T)
        w_plane = zeroed_plane("w_plane", R)

        xo_w = load_words("xo_w", nc.scalar, xo_words[0].rearrange("p n t -> p (n t)"), T, U32)
        w2_rows = load_scale_rows("w2_rows", nc.sync, w2_scales)
        l2 = load_list("l2", offs2)
        w2_raw = load_words("w2_raw", nc.sync, w2_words[0], R, U16)
        load_plane(xo_plane, xo_scales)
        l4 = load_list("l4", offs4)
        sb_t = load_columns("sb_t", nc.sync, sb)
        xt_w = load_words("xt_w", nc.sync, xt_words[0].rearrange("p n t -> p (n t)"), T, U32)
        w_raw = load_words("w_raw", nc.sync, w_words[0], R, U16)
        l1 = load_list("l1", offs)
        load_plane(xt_plane, xt_scales)
        w_rows = load_scale_rows("w_rows", nc.sync, w_scales)
        sg_t = load_columns("sg_t", nc.sync, sg)
        lo_t = load_columns("lo_t", nc.sync, lo)
        l3 = load_list("l3", offs3)
        l5 = load_list("l5", offs5)

        warm_in = sbuf("warm_in", 1, F32)
        warm_out = sbuf("warm_out", 1, F32)
        nc.gpsimd.memset(warm_in[:], 0.0)
        nc.scalar.activation(out=warm_out[:], in_=warm_in[:], func=ACT.Sigmoid)

        w2_d = sbuf("w2_d", R, U16)
        nc.scalar.copy(dealt(w2_d), undealt(w2_raw))
        w2_s = sbuf("w2_s", R, U8)
        xo_gw = sbuf("xo_gw", J, U32)
        xo_gs = sbuf("xo_gs", J, U8)

        def gather_half(dst, window, lst, h):
            nc.vector.tensor_copy(dst[:, h * HALF:(h + 1) * HALF],
                                  window[:].indirect(lst[:, h * HALF // 16:(h + 1) * HALF // 16]))

        def put(name, t, c0, c1):
            acc = psum.tile([P, c1 - c0], F32, name="acc_" + name)
            nc.tensor.matmul_mx(out=acc[:], lhsT=w2_d[:, t * P:(t + 1) * P].bitcast(FP4X4), lhsT_scale=w2_s[:, t * P:(t + 1) * P],
                                rhs=xo_gw[:, c0:c1].bitcast(FP8X4), rhs_scale=xo_gs[:, c0:c1], start=True, stop=True)
            b = sbuf("b_" + name, c1 - c0, F32)
            nc.vector.tensor_copy(b[:], acc[:])
            nc.scalar.activation(out=boards[t][:].indirect(l4[:, c0 // 16:c1 // 16]), in_=b[:], func=ACT.Copy,
                                 scale=sb_t[:, t:t + 1])

        def deal_scales(t):
            nc.vector.tensor_copy(w2_s[:, t * P:(t + 1) * P], w2_plane[:, t::PACK])

        spread(w2_plane, w2_rows)
        gather_half(xo_gs, xo_plane, l2, 0)
        deal_scales(0)
        gather_half(xo_gw, xo_w, l2, 0)
        deal_scales(1)
        put("0a", 0, 0, HALF)
        put("1a", 1, 0, HALF)
        gather_half(xo_gs, xo_plane, l2, 1)
        gather_half(xo_gw, xo_w, l2, 1)
        put("0b", 0, HALF, J)
        put("1b", 1, HALF, J)
        for t in (2, 3):
            deal_scales(t)
            put(str(t), t, 0, J)

        spread(w_plane, w_rows)
        w_d = sbuf("w_d", R, U16)
        w_s = sbuf("w_s", R, U8)
        xt_gw = sbuf("xt_gw", J, U32)
        xt_gs = sbuf("xt_gs", J, U8)
        nc.vector.tensor_copy(xt_gs[:], xt_plane[:].indirect(l1[:]))
        nc.vector.tensor_copy(dealt(w_s), undealt(w_plane))
        nc.vector.tensor_copy(dealt(w_d), undealt(w_raw))
        nc.vector.tensor_copy(xt_gw[:], xt_w[:].indirect(l1[:]))

        z1 = sbuf("z1", PACK * O, BF16)
        z2 = sbuf("z2", PACK * U, BF16)
        acc_a = [psum.tile([P, 2 * J], F32, name="acc_a%d" % i) for i in range(2)]
        for t in range(PACK):
            acc = acc_a[t // 2][:, (t % 2) * J:(t % 2 + 1) * J]
            nc.tensor.matmul_mx(out=acc, lhsT=w_d[:, t * P:(t + 1) * P].bitcast(FP4X4), lhsT_scale=w_s[:, t * P:(t + 1) * P],
                                rhs=xt_gw[:].bitcast(FP8X4), rhs_scale=xt_gs[:], start=True, stop=True)
        for t in range(PACK):
            a = sbuf("a%d" % t, J, F32)
            nc.vector.tensor_copy(a[:], acc_a[t // 2][:, (t % 2) * J:(t % 2 + 1) * J])
            nc.scalar.activation(out=z1[:, t::PACK], in_=a[:].indirect(l3[:]), func=ACT.Sigmoid,
                                 bias=lo_t[:, t:t + 1], scale=sg_t[:, t:t + 1])
        for t in range(PACK):
            nc.scalar.activation(out=z2[:, t::PACK], in_=boards[t][:].indirect(l5[:]), func=ACT.Copy)

        z1_w = sbuf("z1_w", O, U32)
        z1_s = sbuf("z1_s", O, U8)
        z2_w = sbuf("z2_w", U, U32)
        z2_s = sbuf("z2_s", U, U8)
        nc.vector.quantize_mx(out=z1_w[:].bitcast(FP8X4), scales=z1_s[:], in_=z1[:])
        nc.vector.quantize_mx(out=z2_w[:].bitcast(FP8X4), scales=z2_s[:], in_=z2[:])
        acc_y = psum.tile([O, U], F32, name="acc_0a")
        nc.tensor.matmul_mx(out=acc_y[:], lhsT=z1_w[:].bitcast(FP8X4), lhsT_scale=z1_s[:],
                            rhs=z2_w[:].bitcast(FP8X4), rhs_scale=z2_s[:], start=True, stop=True)
        y = sbuf("y", U, F32)
        nc.vector.tensor_copy(y[:], acc_y[:])
        nc.sync.dma_start(out, y[:])
